import numpy as np
import ml_dtypes


def mxq(x, axis, fmt="e4m3"):
    dtype, down = {"e4m3": (ml_dtypes.float8_e4m3fn, 7), "e5m2": (ml_dtypes.float8_e5m2, 14)}[fmt]
    v = np.moveaxis(np.asarray(x, np.float32).astype(ml_dtypes.bfloat16).astype(np.float64), axis, -1)
    blocks = v.reshape(v.shape[:-1] + (-1, 32))
    amax = np.abs(blocks).max(-1, keepdims=True)
    byte = np.maximum(np.where(amax > 0, np.frexp(amax)[1] - 1 + 127, 0) - down, 1)
    scale = np.exp2(byte - 127.0)
    codes = (blocks / scale).astype(np.float32).astype(dtype).astype(np.float64)
    return np.moveaxis((codes * scale).reshape(v.shape), -1, axis)


WIDE = False


def mx_kscale(k):
    if not WIDE:
        return np.ones(k)
    levels = np.array([10, -10, 5, -5, 0])
    if k % 512:
        return np.exp2(np.random.permutation(np.resize(levels, k // 32))).repeat(32)
    a = np.empty((k // 512, 16))
    for p in range(k // 512):
        a[p, :8] = np.random.permutation(np.resize(levels, 8))
        for g in range(8):
            far = levels[np.abs(levels - a[p, g]) >= 10]
            a[p, g + 8] = far[np.random.randint(len(far))]
    return np.exp2(a.ravel()).repeat(32)


def f64(x):
    return np.asarray(x).astype(np.float64)


def striped(idx):
    return np.tile(idx.reshape(-1, 16).T, (8, 1)).astype(np.uint16)


def unstriped(offs):
    return offs[:16].T.reshape(-1).astype(np.int64)


def striped8(idx):
    return np.concatenate([x.reshape(-1, 16).T for x in idx]).astype(np.uint16)


def runs(offs, k):
    lists = np.stack([offs[16 * r : 16 * r + 16].T.reshape(-1) for r in range(8)]).astype(np.int64)
    return lists[np.arange(k) % 512 // 64]


def pack_weight(w):
    k, n = w.shape
    w = f64(np.asarray(w, np.float32).astype(ml_dtypes.bfloat16)).reshape(k // 32, 32, n)
    amax = np.abs(w).max(1)
    byte = np.clip(np.where(amax > 0, np.frexp(amax)[1] - 1 + 127 - 7, 1), 1, 254)
    scaled = (w * np.exp2(127.0 - byte)[:, None, :]).reshape(k, n).astype(np.float32)
    words = np.ascontiguousarray(scaled.reshape(k // 512, 128, 4, n).transpose(0, 1, 3, 2)).astype(ml_dtypes.float8_e4m3fn).view(np.uint8)
    return words, np.ascontiguousarray(byte.astype(np.uint8).reshape(k // 512, 16, n))


def unpack_weight(words, scales):
    g, p, n, _ = words.shape
    vals = np.ascontiguousarray(words).view(ml_dtypes.float8_e4m3fn).astype(np.float64) * np.repeat(np.exp2(scales.astype(np.float64) - 127.0), 8, axis=1)[..., None]
    return vals.transpose(0, 1, 3, 2).reshape(g * 512, n)


K, T, S, N, H, G = 512, 1024, 512, 512, 512, 2048


def setup_inputs():
    n = np.random.standard_normal
    s = mx_kscale(K)[:, None]
    u = mx_kscale(S)
    packed_xT = pack_weight(n((K, T)) * s)
    packed_dT = pack_weight(n((K, G)) / s)
    return {
        "x_words": packed_xT[0],
        "x_scales": packed_xT[1],
        "w1": (n((K, H)) / np.sqrt(K) / s).astype(np.float32),
        "d_words": packed_dT[0],
        "d_scales": packed_dT[1],
        "gn": (np.random.uniform(0.5, 1.5, (H, 1)) * u[:, None]).astype(np.float32),
        "gk": (np.random.uniform(0.5, 1.5, (H, 1)) * u[:, None]).astype(np.float32),
        "w2": (n((H, N)) / np.sqrt(2 * H) / u[:, None]).astype(np.float32),
        "w3": (n((H, N)) / np.sqrt(2 * H) / u[:, None]).astype(np.float32),
        "offs": striped(np.random.permutation(T)[:S]),
        "kidx": striped8(np.random.randint(0, G, (8, H))),
        "two": striped(np.random.permutation(T)[:S]),
        "n1": striped8(np.stack([np.random.permutation(S) for _ in range(8)])),
        "n2": striped(np.random.permutation(S)),
        "n3": striped(np.random.permutation(S)),
        "n4": striped(np.random.permutation(S)),
        "n5": striped(np.random.permutation(S)),
    }


def reference(x_words, x_scales, w1, d_words, d_scales, gn, gk, w2, w3, offs, kidx, two, n1, n2, n3, n4, n5):
    xq = unpack_weight(x_words, x_scales)[:, unstriped(offs)]
    y = mxq(f64(w1), 0, "e4m3").T @ xq
    st = y - (y[np.arange(H)[:, None], runs(n1, H)])
    z = f64(gn) * (st - (0.5 * (st[np.arange(H)[:, None], runs(n1, H)])))
    d_kidx = unpack_weight(d_words, d_scales)[np.arange(K)[:, None], runs(kidx, K)]
    x_two = unpack_weight(x_words, x_scales)[:, unstriped(two)]
    s = 0.0625 * (d_kidx.T @ x_two)
    st2 = s + s[:, unstriped(n2)]
    z2 = f64(gk) * (st2 * (np.tanh(st2[:, unstriped(n3)])))
    h = mxq(f64(w2), 0, "e4m3").T @ mxq(z, 0, "e4m3") + mxq(f64(w3), 0, "e4m3").T @ mxq(z2, 0, "e4m3")
    st3 = np.maximum(h, h[:, unstriped(n4)])
    return st3[:, unstriped(n5)] - (0.5 * h)

@@ -1,0 +1,272 @@
+from contextlib import ExitStack
+
+import concourse.mybir as mybir
+
+K, T, S, N, H, G = 512, 1024, 512, 512, 512, 2048
+FLOPS = 4 * 2 * 512 * 512 * 512
+
+F32 = mybir.dt.float32
+BF16 = mybir.dt.bfloat16
+I32 = mybir.dt.int32
+U32 = mybir.dt.uint32
+U16 = mybir.dt.uint16
+U8 = mybir.dt.uint8
+FP8X4 = mybir.dt.float8_e4m3fn_x4
+ALU = mybir.AluOpType
+ACT = mybir.ActivationFunctionType
+
+P = 128
+PACK = 4
+SPARE = 8
+WIDE_SPARE = 192
+HALF = S // 2
+COLS = HALF // 16
+
+
+def tile_picked_jkeytwicehopphopb_none_p_kernel(
+    tc, x_words, x_scales, w1, d_words, d_scales, gn, gk, w2, w3, offs, kidx, two, n1, n2, n3, n4, n5, out
+):
+    nc = tc.nc
+    with ExitStack() as ctx:
+        lists = ctx.enter_context(tc.tile_pool(name="lists", bufs=1))
+        keep = ctx.enter_context(tc.tile_pool(name="keep", bufs=1))
+        psum = ctx.enter_context(tc.psum_pool(name="psum", bufs=1))
+
+        def load_list(ap, name):
+            tile = lists.tile([P, S // 16], U16, name=name)
+            nc.sync.dma_start(tile[:], ap)
+            return tile
+
+        def sb(name, shape, dtype, slot=None):
+            return keep.tile(shape, dtype, name=name, tag=slot or name, align_bytes=64)
+
+        def four(name, width):
+            return [sb(name + str(t), [P, width], F32) for t in range(PACK)]
+
+        ds = sb("ds", [P, G], U8)
+        nc.vector.memset(ds[:].bitcast(I32), 0)
+        offs_t = load_list(offs, "offs_t")
+        two_t = load_list(two, "two_t")
+        xs = sb("xs", [P, T], U8)
+        for r in range(4):
+            src = x_scales[0, r::4, :].bitcast(I32).unsqueeze(1).broadcast_to([4, 8, T // 4])
+            nc.scalar.dma_start(xs[:].bitcast(I32)[r::4, :], src)
+        w1_rows = w1.rearrange("(p j) c -> p j c", j=PACK)
+        w1_raw = [sb("w1_raw" + str(u), [P, PACK, H // 2], F32) for u in range(2)]
+        nc.sync.dma_start(w1_raw[0][:], w1_rows[:, :, : H // 2])
+        xw = sb("xw", [P, T], U32)
+        nc.sync.dma_start(xw[:].bitcast(I32), x_words[0].rearrange("p n t -> p (n t)").bitcast(I32))
+        kidx_t = load_list(kidx, "kidx_t")
+        for r in range(2):
+            nc.sync.dma_start(ds[:].bitcast(I32)[r::16, :], d_scales[0, r::2, :].bitcast(I32))
+        nc.sync.dma_start(w1_raw[1][:], w1_rows[:, :, H // 2 :])
+        dw = sb("dw", [P, G], U32)
+        nc.sync.dma_start(dw[:].bitcast(I32), d_words[0].rearrange("p n t -> p (n t)").bitcast(I32))
+        n1_t = load_list(n1, "n1_t")
+        w2_raw = sb("w2_raw", [P, PACK, N], F32)
+        nc.sync.dma_start(w2_raw[:], w2.rearrange("(p j) c -> p j c", j=PACK))
+        n2_t = load_list(n2, "n2_t")
+        n3_t = load_list(n3, "n3_t")
+        n4_t = load_list(n4, "n4_t")
+        n5_t = load_list(n5, "n5_t")
+        gn_t = sb("gn_t", [P, PACK], F32)
+        nc.gpsimd.dma_start(gn_t[:], gn.rearrange("(p t) o -> p (t o)", t=PACK))
+        gk_t = sb("gk_t", [P, PACK], F32)
+        nc.gpsimd.dma_start(gk_t[:], gk.rearrange("(p t) o -> p (t o)", t=PACK))
+
+        s_win = four("s_win", S + SPARE)
+        tanh_win = four("tanh_win", S + SPARE)
+        h_win = four("h_win", S + WIDE_SPARE)
+        st3_win = four("st3_win", S + SPARE)
+        for win in s_win + tanh_win + h_win + st3_win:
+            nc.vector.memset(win[:, S:], 0.0)
+
+        def pick(name, table, offsets, dtype, slot=None):
+            picked = sb(name, [P, S], dtype, slot)
+            nc.vector.tensor_copy(picked[:], table[:].indirect(offsets[:]))
+            return picked
+
+        def deal(name, picked, dtype, slot=None):
+            dealt = sb(name, [P, S], dtype, slot)
+            nc.vector.tensor_copy(
+                dealt[:].rearrange("p (t m) -> p m t", t=PACK), picked[:].rearrange("p (m t) -> p m t", t=PACK)
+            )
+            return dealt
+
+        xa_s = pick("xa_s", xs, offs_t, U8)
+        xb_s = pick("xb_s", xs, two_t, U8)
+        xa_w = pick("xa_w", xw, offs_t, U32)
+
+        w1_bf = sb("w1_bf", [P, PACK * H], BF16)
+        w1_view = w1_bf[:].rearrange("p (t m j) -> p m j t", t=PACK, j=PACK)
+        for u in range(2):
+            nc.scalar.copy(w1_view[:, 64 * u : 64 * (u + 1)], w1_raw[u][:].rearrange("p j (m t) -> p m j t", t=PACK))
+
+        def planes_for(name):
+            return sb(name + "_w", [P, S], U32), sb(name + "_s", [P, S], U8)
+
+        def quantize(dst, src, cols):
+            nc.vector.quantize_mx(
+                out=dst[0][:, cols].bitcast(FP8X4),
+                scales=dst[1][:, cols],
+                in_=src[:, PACK * cols.start : PACK * cols.stop],
+            )
+
+        halves = [slice(u * HALF, (u + 1) * HALF) for u in range(2)]
+        whole = slice(0, S)
+        w1_q = planes_for("w1")
+        for cols in halves:
+            quantize(w1_q, w1_bf, cols)
+
+        def product(bank, lhs, t, rhs, cols, start, stop):
+            rows = slice(t * P, (t + 1) * P)
+            nc.tensor.matmul_mx(
+                out=bank[:],
+                lhsT=lhs[0][:, rows].bitcast(FP8X4),
+                lhsT_scale=lhs[1][:, rows],
+                rhs=rhs[0][:, cols].bitcast(FP8X4),
+                rhs_scale=rhs[1][:, cols],
+                start=start,
+                stop=stop,
+            )
+
+        y_ps = [psum.tile([P, S], F32, name="y_ps" + str(t), tag="low" + str(t)) for t in range(PACK)]
+        for t in range(PACK):
+            product(y_ps[t], w1_q, t, (xa_w, xa_s), whole, True, True)
+
+        key_s = deal("key_s", pick("key_s_picked", ds, kidx_t, U8), U8, "w1_raw1")
+        rows = key_s[:].bitcast(I32)
+        for r in range(2):
+            nc.sync.dma_start(rows[2 + r :: 32, :], rows[16 + r :: 32, :])
+        xb_w = pick("xb_w", xw, two_t, U32, "key_s_picked")
+        key_w = deal("key_w", pick("key_w_picked", dw, kidx_t, U32), U32)
+        w3_raw = sb("w3_raw", [P, PACK, N], F32, "dw")
+        nc.sync.dma_start(w3_raw[:], w3.rearrange("(p j) c -> p j c", j=PACK))
+        s_ps = [psum.tile([P, S], F32, name="s_ps" + str(t), tag="high" + str(t)) for t in range(PACK)]
+        for t in range(PACK):
+            product(s_ps[t], (key_w, key_s), t, (xb_w, xb_s), whole, True, True)
+
+        def round_weight(name, raw, copy):
+            rounded = sb(name, [P, PACK * N], BF16)
+            copy(
+                rounded[:].rearrange("p (c i j) -> p c j i", i=4, j=PACK),
+                raw[:].rearrange("p j (c i) -> p c j i", i=4),
+            )
+            return rounded
+
+        def part(offsets, u):
+            return offsets[:, u * COLS : (u + 1) * COLS]
+
+        y_win = four("y_win", S)
+        y_plain = sb("y_plain", [P, PACK, S], F32)
+        st_win = four("st_win", S)
+        st_all = sb("st_all", [P, PACK, S], F32)
+        st_near = sb("st_near", [P, PACK, S], F32)
+        for t in range(PACK):
+            nc.scalar.activation(y_win[t][:], y_ps[t][:], ACT.Copy, scale=gn_t[:, t : t + 1])
+            if t < PACK - 1:
+                nc.scalar.activation(y_plain[:, t, :], y_ps[t][:], ACT.Copy, scale=gn_t[:, t : t + 1])
+            else:
+                nc.sync.dma_start(y_plain[:, t, :], y_win[t][:])
+        for t in range(PACK):
+            for u in range(2):
+                nc.vector.tensor_tensor(
+                    st_win[t][:, halves[u]], y_win[t][:].indirect(part(n1_t, u)), y_plain[:, t, halves[u]], ALU.subtract
+                )
+            nc.sync.dma_start(st_all[:, t, :], st_win[t][:])
+
+        s_plain = sb("s_plain", [P, PACK, S], F32)
+        st2 = sb("st2", [P, PACK, S], F32)
+        st2_gained = sb("st2_gained", [P, PACK, S], F32)
+        tanh_near = sb("tanh_near", [P, PACK, S], F32)
+        for t in range(PACK):
+            nc.scalar.activation(s_win[t][:, :S], s_ps[t][:], ACT.Copy, scale=0.0625)
+            nc.sync.dma_start(s_plain[:, t, :], s_win[t][:, :S])
+        for t in range(PACK):
+            nc.vector.tensor_tensor(st2[:, t, :], s_win[t][:].indirect(n2_t[:]), s_plain[:, t, :], ALU.add)
+        w2_q = planes_for("w2")
+        quantize(w2_q, round_weight("w2_bf", w2_raw, nc.scalar.copy), whole)
+        for t in range(PACK):
+            for u in range(2):
+                nc.scalar.activation(
+                    st_near[:, t, halves[u]], st_win[t][:].indirect(part(n1_t, u)), ACT.Copy, scale=0.5
+                )
+        for t in range(PACK):
+            nc.scalar.activation(tanh_win[t][:, :S], st2[:, t, :], ACT.Tanh)
+
+        def woven(tile, cols):
+            return tile[:, PACK * cols.start : PACK * cols.stop].rearrange("p (c i t) -> p c t i", i=4, t=PACK)
+
+        def planes(tile, cols):
+            return tile[:, :, cols].rearrange("p t (c i) -> p c t i", i=4)
+
+        z_bf = sb("z_bf", [P, PACK * S], BF16)
+        z_q = planes_for("z")
+        for cols in halves:
+            nc.vector.tensor_tensor(woven(z_bf, cols), planes(st_near, cols), planes(st_all, cols), ALU.subtract)
+        for cols in halves:
+            quantize(z_q, z_bf, cols)
+        for t in range(PACK):
+            nc.vector.tensor_scalar(st2_gained[:, t, :], st2[:, t, :], gk_t[:, t : t + 1], None, ALU.mult)
+        w3_q = planes_for("w3")
+        quantize(w3_q, round_weight("w3_bf", w3_raw, nc.vector.tensor_copy), whole)
+
+        z2_q = planes_for("z2")
+        h_ps = [
+            [psum.tile([P, HALF], F32, name="h_ps" + tag + str(t), tag=tag + str(t)) for t in range(PACK)]
+            for tag in ("low", "high")
+        ]
+        for u in range(2):
+            for t in range(PACK):
+                product(h_ps[u][t], w2_q, t, z_q, halves[u], True, False)
+        for u in range(2):
+            for t in range(PACK):
+                nc.scalar.activation(tanh_near[:, t, halves[u]], tanh_win[t][:].indirect(part(n3_t, u)), ACT.Copy)
+        for u in range(2):
+            cols = halves[u]
+            z2_bf = sb("z2_bf", [P, PACK * HALF], BF16)
+            nc.vector.tensor_tensor(
+                woven(z2_bf, halves[0]), planes(tanh_near, cols), planes(st2_gained, cols), ALU.mult
+            )
+            nc.vector.quantize_mx(out=z2_q[0][:, cols].bitcast(FP8X4), scales=z2_q[1][:, cols], in_=z2_bf[:])
+            for t in range(PACK):
+                product(h_ps[u][t], w3_q, t, z2_q, cols, False, True)
+            for t in range(PACK):
+                if u == 1 and t == 1:
+                    nc.vector.tensor_scalar(h_win[t][:, cols], h_ps[u][t][:], -0.5, None, ALU.mult)
+                else:
+                    nc.scalar.activation(h_win[t][:, cols], h_ps[u][t][:], ACT.Copy, scale=-0.5)
+
+        h_near = sb("h_near", [P, PACK, S], F32)
+        st3_near = sb("st3_near", [P, 2, S], F32)
+        result = four("result", S)
+
+        def store(t):
+            nc.sync.dma_start(out[t * P : (t + 1) * P, :], result[t][:])
+
+        def larger(t):
+            nc.vector.scalar_tensor_tensor(st3_win[t][:, :S], h_win[t][:, :S], -2.0, h_near[:, t, :], ALU.mult, ALU.max)
+
+        def fused_end(t):
+            nc.vector.tensor_tensor(result[t][:], st3_win[t][:].indirect(n5_t[:]), h_win[t][:, :S], ALU.add)
+            store(t)
+
+        for t in range(PACK):
+            if t == 1:
+                nc.vector.tensor_copy(h_near[:, t, :], h_win[t][:].indirect(n4_t[:]))
+            else:
+                nc.scalar.activation(h_near[:, t, :], h_win[t][:].indirect(n4_t[:]), ACT.Copy, scale=-2.0)
+        larger(0)
+        for u in range(2):
+            nc.vector.scalar_tensor_tensor(
+                st3_win[1][:, halves[u]], h_near[:, 1, halves[u]], -2.0, h_ps[u][1][:], ALU.mult, ALU.max
+            )
+        larger(2)
+        fused_end(0)
+        larger(3)
+        fused_end(1)
+        for t in (2, 3):
+            nc.scalar.activation(st3_near[:, t - 2, :], st3_win[t][:].indirect(n5_t[:]), ACT.Copy)
+        for t in (2, 3):
+            nc.vector.tensor_tensor(result[t][:], st3_near[:, t - 2, :], h_win[t][:, :S], ALU.add)
+            store(t)

@@ -43,30 +43,35 @@ def tile_picked_jkeytwicehopphopb_none_p_kernel(
         def four(name, width):
             return [sb(name + str(t), [P, width], F32) for t in range(PACK)]
 
+        xs = sb("xs", [P, T], U8)
         ds = sb("ds", [P, G], U8)
         nc.vector.memset(ds[:].bitcast(I32), 0)
         offs_t = load_list(offs, "offs_t")
         two_t = load_list(two, "two_t")
-        xs = sb("xs", [P, T], U8)
-        for r in range(4):
-            src = x_scales[0, r::4, :].bitcast(I32).unsqueeze(1).broadcast_to([4, 8, T // 4])
-            nc.scalar.dma_start(xs[:].bitcast(I32)[r::4, :], src)
-        w1_rows = w1.rearrange("(p j) c -> p j c", j=PACK)
-        w1_raw = [sb("w1_raw" + str(u), [P, PACK, H // 2], F32) for u in range(2)]
-        nc.sync.dma_start(w1_raw[0][:], w1_rows[:, :, : H // 2])
+        for q in range(4):
+            src = x_scales[0, 4 * q : 4 * q + 4, :].bitcast(I32).unsqueeze(0).broadcast_to([8, 4, T // 4])
+            nc.sync.dma_start(xs[:].bitcast(I32)[32 * q : 32 * (q + 1), :], src)
         xw = sb("xw", [P, T], U32)
         nc.sync.dma_start(xw[:].bitcast(I32), x_words[0].rearrange("p n t -> p (n t)").bitcast(I32))
+
+        def load_half(name, w, u):
+            raw = sb(name + str(u), [P, PACK, HALF], F32)
+            nc.sync.dma_start(raw[:], w.rearrange("(p j) c -> p j c", j=PACK)[:, :, u * HALF : (u + 1) * HALF])
+            return raw
+
+        w1_raw = [load_half("w1_raw", w1, u) for u in range(2)]
         kidx_t = load_list(kidx, "kidx_t")
         for r in range(2):
             nc.sync.dma_start(ds[:].bitcast(I32)[r::16, :], d_scales[0, r::2, :].bitcast(I32))
-        nc.sync.dma_start(w1_raw[1][:], w1_rows[:, :, H // 2 :])
+        w2_raw = [load_half("w2_raw", w2, 0)]
         dw = sb("dw", [P, G], U32)
         nc.sync.dma_start(dw[:].bitcast(I32), d_words[0].rearrange("p n t -> p (n t)").bitcast(I32))
         n1_t = load_list(n1, "n1_t")
-        w2_raw = sb("w2_raw", [P, PACK, N], F32)
-        nc.sync.dma_start(w2_raw[:], w2.rearrange("(p j) c -> p j c", j=PACK))
+        w2_raw.append(load_half("w2_raw", w2, 1))
         n2_t = load_list(n2, "n2_t")
         n3_t = load_list(n3, "n3_t")
+        w3_raw = sb("w3_raw", [P, PACK, N], F32)
+        nc.sync.dma_start(w3_raw[:], w3.rearrange("(p j) c -> p j c", j=PACK))
         n4_t = load_list(n4, "n4_t")
         n5_t = load_list(n5, "n5_t")
         gn_t = sb("gn_t", [P, PACK], F32)
@@ -80,6 +85,9 @@ def tile_picked_jkeytwicehopphopb_none_p_kernel(
         st3_win = four("st3_win", S + SPARE)
         for win in s_win + tanh_win + h_win + st3_win:
             nc.vector.memset(win[:, S:], 0.0)
+
+        gk_16th = sb("gk_16th", [P, PACK], F32)
+        nc.gpsimd.tensor_scalar(gk_16th[:], gk_t[:], 0.0625, 0.0, ALU.mult, ALU.add)
 
         def pick(name, table, offsets, dtype, slot=None):
             picked = sb(name, [P, S], dtype, slot)
@@ -96,6 +104,7 @@ def tile_picked_jkeytwicehopphopb_none_p_kernel(
         xa_s = pick("xa_s", xs, offs_t, U8)
         xb_s = pick("xb_s", xs, two_t, U8)
         xa_w = pick("xa_w", xw, offs_t, U32)
+        xb_w = pick("xb_w", xw, two_t, U32)
 
         w1_bf = sb("w1_bf", [P, PACK * H], BF16)
         w1_view = w1_bf[:].rearrange("p (t m j) -> p m j t", t=PACK, j=PACK)
@@ -134,82 +143,81 @@ def tile_picked_jkeytwicehopphopb_none_p_kernel(
         for t in range(PACK):
             product(y_ps[t], w1_q, t, (xa_w, xa_s), whole, True, True)
 
-        key_s = deal("key_s", pick("key_s_picked", ds, kidx_t, U8), U8, "w1_raw1")
+        def woven(tile, cols):
+            return tile[:, PACK * cols.start : PACK * cols.stop].rearrange("p (c i t) -> p c t i", i=4, t=PACK)
+
+        def planes(view):
+            return view.rearrange("p t (c i) -> p c t i", i=4)
+
+        w2_bf = sb("w2_bf", [P, PACK * N], BF16)
+        nc.scalar.copy(woven(w2_bf, halves[0]), planes(w2_raw[0][:]))
+
+        key_s_picked = pick("key_s_picked", ds, kidx_t, U8, "w1_raw1")
+        key_w_picked = pick("key_w_picked", dw, kidx_t, U32)
+        key_s = deal("key_s", key_s_picked, U8)
         rows = key_s[:].bitcast(I32)
         for r in range(2):
             nc.sync.dma_start(rows[2 + r :: 32, :], rows[16 + r :: 32, :])
-        xb_w = pick("xb_w", xw, two_t, U32, "key_s_picked")
-        key_w = deal("key_w", pick("key_w_picked", dw, kidx_t, U32), U32)
-        w3_raw = sb("w3_raw", [P, PACK, N], F32, "dw")
-        nc.sync.dma_start(w3_raw[:], w3.rearrange("(p j) c -> p j c", j=PACK))
+        key_w = deal("key_w", key_w_picked, U32)
+        gk_safe = sb("gk_safe", [P, PACK], F32, "key_w_picked")
+        nc.vector.scalar_tensor_tensor(gk_safe[:], gk_t[:], 0.0, gk_t[:], ALU.is_equal, ALU.add)
+        gk_inv = sb("gk_inv", [P, PACK], F32)
+        nc.vector.reciprocal(gk_inv[:], gk_safe[:])
+        gk_undo = sb("gk_undo", [P, PACK], F32)
+        nc.gpsimd.tensor_scalar(gk_undo[:], gk_inv[:], 3.0e38, -3.0e38, ALU.min, ALU.max)
+
         s_ps = [psum.tile([P, S], F32, name="s_ps" + str(t), tag="high" + str(t)) for t in range(PACK)]
         for t in range(PACK):
             product(s_ps[t], (key_w, key_s), t, (xb_w, xb_s), whole, True, True)
-
-        def round_weight(name, raw, copy):
-            rounded = sb(name, [P, PACK * N], BF16)
-            copy(
-                rounded[:].rearrange("p (c i j) -> p c j i", i=4, j=PACK),
-                raw[:].rearrange("p j (c i) -> p c j i", i=4),
-            )
-            return rounded
 
         def part(offsets, u):
             return offsets[:, u * COLS : (u + 1) * COLS]
 
         y_win = four("y_win", S)
         y_plain = sb("y_plain", [P, PACK, S], F32)
-        st_win = four("st_win", S)
-        st_all = sb("st_all", [P, PACK, S], F32)
-        st_near = sb("st_near", [P, PACK, S], F32)
+        mix_win = four("mix_win", S)
         for t in range(PACK):
             nc.scalar.activation(y_win[t][:], y_ps[t][:], ACT.Copy, scale=gn_t[:, t : t + 1])
-            if t < PACK - 1:
-                nc.scalar.activation(y_plain[:, t, :], y_ps[t][:], ACT.Copy, scale=gn_t[:, t : t + 1])
-            else:
-                nc.sync.dma_start(y_plain[:, t, :], y_win[t][:])
+            nc.scalar.activation(y_plain[:, t, :], y_ps[t][:], ACT.Copy, scale=gn_t[:, t : t + 1])
         for t in range(PACK):
             for u in range(2):
                 nc.vector.tensor_tensor(
-                    st_win[t][:, halves[u]], y_win[t][:].indirect(part(n1_t, u)), y_plain[:, t, halves[u]], ALU.subtract
+                    mix_win[t][:, halves[u]], y_win[t][:].indirect(part(n1_t, u)), y_plain[:, t, halves[u]], ALU.subtract
                 )
-            nc.sync.dma_start(st_all[:, t, :], st_win[t][:])
 
         s_plain = sb("s_plain", [P, PACK, S], F32)
         st2 = sb("st2", [P, PACK, S], F32)
-        st2_gained = sb("st2_gained", [P, PACK, S], F32)
         tanh_near = sb("tanh_near", [P, PACK, S], F32)
         for t in range(PACK):
-            nc.scalar.activation(s_win[t][:, :S], s_ps[t][:], ACT.Copy, scale=0.0625)
+            nc.scalar.activation(s_win[t][:, :S], s_ps[t][:], ACT.Copy, scale=gk_16th[:, t : t + 1])
             nc.sync.dma_start(s_plain[:, t, :], s_win[t][:, :S])
+        nc.scalar.copy(woven(w2_bf, halves[1]), planes(w2_raw[1][:]))
         for t in range(PACK):
             nc.vector.tensor_tensor(st2[:, t, :], s_win[t][:].indirect(n2_t[:]), s_plain[:, t, :], ALU.add)
-        w2_q = planes_for("w2")
-        quantize(w2_q, round_weight("w2_bf", w2_raw, nc.scalar.copy), whole)
+        mix_near = sb("mix_near", [P, PACK, S], F32, "key_w")
+        mix_plain = sb("mix_plain", [P, PACK, S], F32, "s_win0")
+        for t in range(PACK):
+            nc.sync.dma_start(mix_plain[:, t, :], mix_win[t][:])
         for t in range(PACK):
             for u in range(2):
                 nc.scalar.activation(
-                    st_near[:, t, halves[u]], st_win[t][:].indirect(part(n1_t, u)), ACT.Copy, scale=0.5
+                    mix_near[:, t, halves[u]], mix_win[t][:].indirect(part(n1_t, u)), ACT.Copy, scale=0.5
                 )
+        w2_q = planes_for("w2")
+        quantize(w2_q, w2_bf, whole)
         for t in range(PACK):
-            nc.scalar.activation(tanh_win[t][:, :S], st2[:, t, :], ACT.Tanh)
+            nc.scalar.activation(tanh_win[t][:, :S], st2[:, t, :], ACT.Tanh, scale=gk_undo[:, t : t + 1])
 
-        def woven(tile, cols):
-            return tile[:, PACK * cols.start : PACK * cols.stop].rearrange("p (c i t) -> p c t i", i=4, t=PACK)
-
-        def planes(tile, cols):
-            return tile[:, :, cols].rearrange("p t (c i) -> p c t i", i=4)
-
-        z_bf = sb("z_bf", [P, PACK * S], BF16)
+        z_bf = sb("z_bf", [P, PACK * S], BF16, "s_plain")
         z_q = planes_for("z")
         for cols in halves:
-            nc.vector.tensor_tensor(woven(z_bf, cols), planes(st_near, cols), planes(st_all, cols), ALU.subtract)
+            nc.vector.tensor_tensor(woven(z_bf, cols), planes(mix_near[:, :, cols]), planes(mix_plain[:, :, cols]), ALU.subtract)
         for cols in halves:
             quantize(z_q, z_bf, cols)
-        for t in range(PACK):
-            nc.vector.tensor_scalar(st2_gained[:, t, :], st2[:, t, :], gk_t[:, t : t + 1], None, ALU.mult)
+        w3_bf = sb("w3_bf", [P, PACK * N], BF16)
+        nc.vector.tensor_copy(woven(w3_bf, whole), planes(w3_raw[:]))
         w3_q = planes_for("w3")
-        quantize(w3_q, round_weight("w3_bf", w3_raw, nc.vector.tensor_copy), whole)
+        quantize(w3_q, w3_bf, whole)
 
         z2_q = planes_for("z2")
         h_ps = [
@@ -224,9 +232,9 @@ def tile_picked_jkeytwicehopphopb_none_p_kernel(
                 nc.scalar.activation(tanh_near[:, t, halves[u]], tanh_win[t][:].indirect(part(n3_t, u)), ACT.Copy)
         for u in range(2):
             cols = halves[u]
-            z2_bf = sb("z2_bf", [P, PACK * HALF], BF16)
+            z2_bf = sb("z2_bf", [P, PACK * HALF], BF16, "s_plain")
             nc.vector.tensor_tensor(
-                woven(z2_bf, halves[0]), planes(tanh_near, cols), planes(st2_gained, cols), ALU.mult
+                woven(z2_bf, halves[0]), planes(tanh_near[:, :, cols]), planes(st2[:, :, cols]), ALU.mult
             )
             nc.vector.quantize_mx(out=z2_q[0][:, cols].bitcast(FP8X4), scales=z2_q[1][:, cols], in_=z2_bf[:])
             for t in range(PACK):
@@ -261,12 +269,12 @@ def tile_picked_jkeytwicehopphopb_none_p_kernel(
             nc.vector.scalar_tensor_tensor(
                 st3_win[1][:, halves[u]], h_near[:, 1, halves[u]], -2.0, h_ps[u][1][:], ALU.mult, ALU.max
             )
-        larger(2)
         fused_end(0)
+        larger(2)
         larger(3)
-        fused_end(1)
-        for t in (2, 3):
-            nc.scalar.activation(st3_near[:, t - 2, :], st3_win[t][:].indirect(n5_t[:]), ACT.Copy)
-        for t in (2, 3):
-            nc.vector.tensor_tensor(result[t][:], st3_near[:, t - 2, :], h_win[t][:, :S], ALU.add)
+        fused_end(2)
+        for t in (1, 3):
+            nc.scalar.activation(st3_near[:, t // 2, :], st3_win[t][:].indirect(n5_t[:]), ACT.Copy)
+        for t in (1, 3):
+            nc.vector.tensor_tensor(result[t][:], st3_near[:, t // 2, :], h_win[t][:, :S], ALU.add)
             store(t)

@@ -70,8 +70,6 @@ def tile_picked_jkeytwicehopphopb_none_p_kernel(
         w2_raw.append(load_half("w2_raw", w2, 1))
         n2_t = load_list(n2, "n2_t")
         n3_t = load_list(n3, "n3_t")
-        w3_raw = sb("w3_raw", [P, PACK, N], F32)
-        nc.sync.dma_start(w3_raw[:], w3.rearrange("(p j) c -> p j c", j=PACK))
         n4_t = load_list(n4, "n4_t")
         n5_t = load_list(n5, "n5_t")
         gn_t = sb("gn_t", [P, PACK], F32)
@@ -81,8 +79,11 @@ def tile_picked_jkeytwicehopphopb_none_p_kernel(
 
         s_win = four("s_win", S + SPARE)
         tanh_win = four("tanh_win", S + SPARE)
-        h_win = four("h_win", S + WIDE_SPARE)
+        h_win = [sb("h_win" + str(t), [P, S + (WIDE_SPARE if t == 1 else SPARE)], F32) for t in range(PACK)]
         st3_win = four("st3_win", S + SPARE)
+        y_win = four("y_win", 2 * S)
+        for win in y_win:
+            nc.gpsimd.memset(win[:, S:], 0.0)
         for win in s_win + tanh_win + h_win + st3_win:
             nc.vector.memset(win[:, S:], 0.0)
 
@@ -104,7 +105,7 @@ def tile_picked_jkeytwicehopphopb_none_p_kernel(
         xa_s = pick("xa_s", xs, offs_t, U8)
         xb_s = pick("xb_s", xs, two_t, U8)
         xa_w = pick("xa_w", xw, offs_t, U32)
-        xb_w = pick("xb_w", xw, two_t, U32)
+        key_s_picked = pick("key_s_picked", ds, kidx_t, U8)
 
         w1_bf = sb("w1_bf", [P, PACK * H], BF16)
         w1_view = w1_bf[:].rearrange("p (t m j) -> p m j t", t=PACK, j=PACK)
@@ -152,12 +153,15 @@ def tile_picked_jkeytwicehopphopb_none_p_kernel(
         w2_bf = sb("w2_bf", [P, PACK * N], BF16)
         nc.scalar.copy(woven(w2_bf, halves[0]), planes(w2_raw[0][:]))
 
-        key_s_picked = pick("key_s_picked", ds, kidx_t, U8, "w1_raw1")
-        key_w_picked = pick("key_w_picked", dw, kidx_t, U32)
-        key_s = deal("key_s", key_s_picked, U8)
+        key_s = sb("key_s", [P, S], U8, "w1_raw1")
+        nc.vector.tensor_copy(
+            key_s[:].rearrange("p (t m) -> p t m", t=PACK), key_s_picked[:].rearrange("p (m t) -> p t m", t=PACK)
+        )
         rows = key_s[:].bitcast(I32)
         for r in range(2):
             nc.sync.dma_start(rows[2 + r :: 32, :], rows[16 + r :: 32, :])
+        xb_w = pick("xb_w", xw, two_t, U32, "w1_bf")
+        key_w_picked = pick("key_w_picked", dw, kidx_t, U32)
         key_w = deal("key_w", key_w_picked, U32)
         gk_safe = sb("gk_safe", [P, PACK], F32, "key_w_picked")
         nc.vector.scalar_tensor_tensor(gk_safe[:], gk_t[:], 0.0, gk_t[:], ALU.is_equal, ALU.add)
@@ -173,17 +177,16 @@ def tile_picked_jkeytwicehopphopb_none_p_kernel(
         def part(offsets, u):
             return offsets[:, u * COLS : (u + 1) * COLS]
 
-        y_win = four("y_win", S)
         y_plain = sb("y_plain", [P, PACK, S], F32)
         mix_win = four("mix_win", S)
         for t in range(PACK):
-            nc.scalar.activation(y_win[t][:], y_ps[t][:], ACT.Copy, scale=gn_t[:, t : t + 1])
-            nc.scalar.activation(y_plain[:, t, :], y_ps[t][:], ACT.Copy, scale=gn_t[:, t : t + 1])
-        for t in range(PACK):
-            for u in range(2):
-                nc.vector.tensor_tensor(
-                    mix_win[t][:, halves[u]], y_win[t][:].indirect(part(n1_t, u)), y_plain[:, t, halves[u]], ALU.subtract
-                )
+            nc.scalar.activation(y_win[t][:, :S], y_ps[t][:], ACT.Copy, scale=gn_t[:, t : t + 1])
+            if t < 2:
+                nc.sync.dma_start(y_plain[:, t, :], y_win[t][:, :S])
+            else:
+                nc.scalar.activation(y_plain[:, t, :], y_ps[t][:], ACT.Copy, scale=gn_t[:, t : t + 1])
+        for t in (2, 3, 0, 1):
+            nc.vector.tensor_tensor(mix_win[t][:], y_win[t][:].indirect(n1_t[:]), y_plain[:, t, :], ALU.subtract)
 
         s_plain = sb("s_plain", [P, PACK, S], F32)
         st2 = sb("st2", [P, PACK, S], F32)
@@ -191,30 +194,35 @@ def tile_picked_jkeytwicehopphopb_none_p_kernel(
         for t in range(PACK):
             nc.scalar.activation(s_win[t][:, :S], s_ps[t][:], ACT.Copy, scale=gk_16th[:, t : t + 1])
             nc.sync.dma_start(s_plain[:, t, :], s_win[t][:, :S])
+        mix_plain = sb("mix_plain", [P, PACK, S], F32, "gk_16th")
+        for t in (2, 3, 0, 1):
+            nc.sync.dma_start(mix_plain[:, t, :], mix_win[t][:])
         nc.scalar.copy(woven(w2_bf, halves[1]), planes(w2_raw[1][:]))
         for t in range(PACK):
             nc.vector.tensor_tensor(st2[:, t, :], s_win[t][:].indirect(n2_t[:]), s_plain[:, t, :], ALU.add)
         mix_near = sb("mix_near", [P, PACK, S], F32, "key_w")
-        mix_plain = sb("mix_plain", [P, PACK, S], F32, "s_win0")
-        for t in range(PACK):
-            nc.sync.dma_start(mix_plain[:, t, :], mix_win[t][:])
-        for t in range(PACK):
+        for t in (2, 3, 0, 1):
             for u in range(2):
                 nc.scalar.activation(
                     mix_near[:, t, halves[u]], mix_win[t][:].indirect(part(n1_t, u)), ACT.Copy, scale=0.5
                 )
+        w3_raw = sb("w3_raw", [P, PACK, N], F32, "s_win0")
+        nc.sync.dma_start(w3_raw[:], w3.rearrange("(p j) c -> p j c", j=PACK))
         w2_q = planes_for("w2")
         quantize(w2_q, w2_bf, whole)
         for t in range(PACK):
             nc.scalar.activation(tanh_win[t][:, :S], st2[:, t, :], ACT.Tanh, scale=gk_undo[:, t : t + 1])
 
-        z_bf = sb("z_bf", [P, PACK * S], BF16, "s_plain")
+        z_bf = [sb("z_bf" + str(u), [P, PACK * HALF], BF16, "s_win" + str(2 + u)) for u in range(2)]
         z_q = planes_for("z")
-        for cols in halves:
-            nc.vector.tensor_tensor(woven(z_bf, cols), planes(mix_near[:, :, cols]), planes(mix_plain[:, :, cols]), ALU.subtract)
-        for cols in halves:
-            quantize(z_q, z_bf, cols)
-        w3_bf = sb("w3_bf", [P, PACK * N], BF16)
+        for u in range(2):
+            cols = halves[u]
+            nc.vector.tensor_tensor(
+                woven(z_bf[u], halves[0]), planes(mix_near[:, :, cols]), planes(mix_plain[:, :, cols]), ALU.subtract
+            )
+        for u in range(2):
+            nc.vector.quantize_mx(out=z_q[0][:, halves[u]].bitcast(FP8X4), scales=z_q[1][:, halves[u]], in_=z_bf[u][:])
+        w3_bf = sb("w3_bf", [P, PACK * N], BF16, "gk_16th")
         nc.vector.tensor_copy(woven(w3_bf, whole), planes(w3_raw[:]))
         w3_q = planes_for("w3")
         quantize(w3_q, w3_bf, whole)
@@ -232,7 +240,7 @@ def tile_picked_jkeytwicehopphopb_none_p_kernel(
                 nc.scalar.activation(tanh_near[:, t, halves[u]], tanh_win[t][:].indirect(part(n3_t, u)), ACT.Copy)
         for u in range(2):
             cols = halves[u]
-            z2_bf = sb("z2_bf", [P, PACK * HALF], BF16, "s_plain")
+            z2_bf = sb("z2_bf" + str(u), [P, PACK * HALF], BF16, "s_win" + str(2 + u))
             nc.vector.tensor_tensor(
                 woven(z2_bf, halves[0]), planes(tanh_near[:, :, cols]), planes(st2[:, :, cols]), ALU.mult
             )
@@ -275,6 +283,8 @@ def tile_picked_jkeytwicehopphopb_none_p_kernel(
         fused_end(2)
         for t in (1, 3):
             nc.scalar.activation(st3_near[:, t // 2, :], st3_win[t][:].indirect(n5_t[:]), ACT.Copy)
-        for t in (1, 3):
-            nc.vector.tensor_tensor(result[t][:], st3_near[:, t // 2, :], h_win[t][:, :S], ALU.add)
-            store(t)
+        nc.vector.tensor_tensor(result[1][:], st3_near[:, 0, :], h_win[1][:, :S], ALU.add)
+        store(1)
+        for cols in halves:
+            nc.vector.tensor_tensor(result[3][:, cols], st3_near[:, 1, cols], h_win[3][:, cols], ALU.add)
+            nc.sync.dma_start(out[3 * P :, cols], result[3][:, cols])

@@ -81,9 +81,7 @@ def tile_picked_jkeytwicehopphopb_none_p_kernel(
         tanh_win = four("tanh_win", S + SPARE)
         h_win = [sb("h_win" + str(t), [P, S + (WIDE_SPARE if t == 1 else SPARE)], F32) for t in range(PACK)]
         st3_win = four("st3_win", S + SPARE)
-        y_win = four("y_win", 2 * S)
-        for win in y_win:
-            nc.gpsimd.memset(win[:, S:], 0.0)
+        y_win = four("y_win", S)
         for win in s_win + tanh_win + h_win + st3_win:
             nc.vector.memset(win[:, S:], 0.0)
 
@@ -186,7 +184,10 @@ def tile_picked_jkeytwicehopphopb_none_p_kernel(
             else:
                 nc.scalar.activation(y_plain[:, t, :], y_ps[t][:], ACT.Copy, scale=gn_t[:, t : t + 1])
         for t in (2, 3, 0, 1):
-            nc.vector.tensor_tensor(mix_win[t][:], y_win[t][:].indirect(n1_t[:]), y_plain[:, t, :], ALU.subtract)
+            for u in range(2):
+                nc.vector.tensor_tensor(
+                    mix_win[t][:, halves[u]], y_win[t][:].indirect(part(n1_t, u)), y_plain[:, t, halves[u]], ALU.subtract
+                )
 
         s_plain = sb("s_plain", [P, PACK, S], F32)
         st2 = sb("st2", [P, PACK, S], F32)

from contextlib import ExitStack

import concourse.mybir as mybir

K, T, S, N, H, G = 512, 1024, 512, 512, 512, 2048
FLOPS = 4 * 2 * 512 * 512 * 512

F32 = mybir.dt.float32
BF16 = mybir.dt.bfloat16
I32 = mybir.dt.int32
U32 = mybir.dt.uint32
U16 = mybir.dt.uint16
U8 = mybir.dt.uint8
FP8X4 = mybir.dt.float8_e4m3fn_x4
ALU = mybir.AluOpType
ACT = mybir.ActivationFunctionType

P = 128
PACK = 4
SPARE = 8
WIDE_SPARE = 192
HALF = S // 2
COLS = HALF // 16


def tile_picked_jkeytwicehopphopb_none_p_kernel(
    tc, x_words, x_scales, w1, d_words, d_scales, gn, gk, w2, w3, offs, kidx, two, n1, n2, n3, n4, n5, out
):
    nc = tc.nc
    with ExitStack() as ctx:
        lists = ctx.enter_context(tc.tile_pool(name="lists", bufs=1))
        keep = ctx.enter_context(tc.tile_pool(name="keep", bufs=1))
        psum = ctx.enter_context(tc.psum_pool(name="psum", bufs=1))

        def load_list(ap, name):
            tile = lists.tile([P, S // 16], U16, name=name)
            nc.sync.dma_start(tile[:], ap)
            return tile

        def sb(name, shape, dtype, slot=None):
            return keep.tile(shape, dtype, name=name, tag=slot or name, align_bytes=64)

        def four(name, width):
            return [sb(name + str(t), [P, width], F32) for t in range(PACK)]

        xs = sb("xs", [P, T], U8)
        ds = sb("ds", [P, G], U8)
        nc.vector.memset(ds[:].bitcast(I32), 0)
        offs_t = load_list(offs, "offs_t")
        two_t = load_list(two, "two_t")
        for q in range(4):
            src = x_scales[0, 4 * q : 4 * q + 4, :].bitcast(I32).unsqueeze(0).broadcast_to([8, 4, T // 4])
            nc.sync.dma_start(xs[:].bitcast(I32)[32 * q : 32 * (q + 1), :], src)
        xw = sb("xw", [P, T], U32)
        nc.sync.dma_start(xw[:].bitcast(I32), x_words[0].rearrange("p n t -> p (n t)").bitcast(I32))

        def load_half(name, w, u):
            raw = sb(name + str(u), [P, PACK, HALF], F32)
            nc.sync.dma_start(raw[:], w.rearrange("(p j) c -> p j c", j=PACK)[:, :, u * HALF : (u + 1) * HALF])
            return raw

        w1_raw = [load_half("w1_raw", w1, u) for u in range(2)]
        kidx_t = load_list(kidx, "kidx_t")
        for r in range(2):
            nc.sync.dma_start(ds[:].bitcast(I32)[r::16, :], d_scales[0, r::2, :].bitcast(I32))
        w2_raw = [load_half("w2_raw", w2, 0)]
        dw = sb("dw", [P, G], U32)
        nc.sync.dma_start(dw[:].bitcast(I32), d_words[0].rearrange("p n t -> p (n t)").bitcast(I32))
        n1_t = load_list(n1, "n1_t")
        w2_raw.append(load_half("w2_raw", w2, 1))
        n2_t = load_list(n2, "n2_t")
        n3_t = load_list(n3, "n3_t")
        n4_t = load_list(n4, "n4_t")
        n5_t = load_list(n5, "n5_t")
        gn_t = sb("gn_t", [P, PACK], F32)
        nc.gpsimd.dma_start(gn_t[:], gn.rearrange("(p t) o -> p (t o)", t=PACK))
        gk_t = sb("gk_t", [P, PACK], F32)
        nc.gpsimd.dma_start(gk_t[:], gk.rearrange("(p t) o -> p (t o)", t=PACK))

        s_win = four("s_win", S + SPARE)
        tanh_win = four("tanh_win", S + SPARE)
        h_win = [sb("h_win" + str(t), [P, S + (WIDE_SPARE if t == 1 else SPARE)], F32) for t in range(PACK)]
        st3_win = four("st3_win", S + SPARE)
        y_win = four("y_win", S)
        for win in s_win + tanh_win + h_win + st3_win:
            nc.vector.memset(win[:, S:], 0.0)

        gk_16th = sb("gk_16th", [P, PACK], F32)
        nc.gpsimd.tensor_scalar(gk_16th[:], gk_t[:], 0.0625, 0.0, ALU.mult, ALU.add)

        def pick(name, table, offsets, dtype, slot=None):
            picked = sb(name, [P, S], dtype, slot)
            nc.vector.tensor_copy(picked[:], table[:].indirect(offsets[:]))
            return picked

        def deal(name, picked, dtype, slot=None):
            dealt = sb(name, [P, S], dtype, slot)
            nc.vector.tensor_copy(
                dealt[:].rearrange("p (t m) -> p m t", t=PACK), picked[:].rearrange("p (m t) -> p m t", t=PACK)
            )
            return dealt

        xa_s = pick("xa_s", xs, offs_t, U8)
        xb_s = pick("xb_s", xs, two_t, U8)
        xa_w = pick("xa_w", xw, offs_t, U32)
        key_s_picked = pick("key_s_picked", ds, kidx_t, U8)

        w1_bf = sb("w1_bf", [P, PACK * H], BF16)
        w1_view = w1_bf[:].rearrange("p (t m j) -> p m j t", t=PACK, j=PACK)
        for u in range(2):
            nc.scalar.copy(w1_view[:, 64 * u : 64 * (u + 1)], w1_raw[u][:].rearrange("p j (m t) -> p m j t", t=PACK))

        def planes_for(name):
            return sb(name + "_w", [P, S], U32), sb(name + "_s", [P, S], U8)

        def quantize(dst, src, cols):
            nc.vector.quantize_mx(
                out=dst[0][:, cols].bitcast(FP8X4),
                scales=dst[1][:, cols],
                in_=src[:, PACK * cols.start : PACK * cols.stop],
            )

        halves = [slice(u * HALF, (u + 1) * HALF) for u in range(2)]
        whole = slice(0, S)
        w1_q = planes_for("w1")
        for cols in halves:
            quantize(w1_q, w1_bf, cols)

        def product(bank, lhs, t, rhs, cols, start, stop):
            rows = slice(t * P, (t + 1) * P)
            nc.tensor.matmul_mx(
                out=bank[:],
                lhsT=lhs[0][:, rows].bitcast(FP8X4),
                lhsT_scale=lhs[1][:, rows],
                rhs=rhs[0][:, cols].bitcast(FP8X4),
                rhs_scale=rhs[1][:, cols],
                start=start,
                stop=stop,
            )

        y_ps = [psum.tile([P, S], F32, name="y_ps" + str(t), tag="low" + str(t)) for t in range(PACK)]
        for t in range(PACK):
            product(y_ps[t], w1_q, t, (xa_w, xa_s), whole, True, True)

        def woven(tile, cols):
            return tile[:, PACK * cols.start : PACK * cols.stop].rearrange("p (c i t) -> p c t i", i=4, t=PACK)

        def planes(view):
            return view.rearrange("p t (c i) -> p c t i", i=4)

        w2_bf = sb("w2_bf", [P, PACK * N], BF16)
        nc.scalar.copy(woven(w2_bf, halves[0]), planes(w2_raw[0][:]))

        key_s = sb("key_s", [P, S], U8, "w1_raw1")
        nc.vector.tensor_copy(
            key_s[:].rearrange("p (t m) -> p t m", t=PACK), key_s_picked[:].rearrange("p (m t) -> p t m", t=PACK)
        )
        rows = key_s[:].bitcast(I32)
        for r in range(2):
            nc.sync.dma_start(rows[2 + r :: 32, :], rows[16 + r :: 32, :])
        xb_w = pick("xb_w", xw, two_t, U32, "w1_bf")
        key_w_picked = pick("key_w_picked", dw, kidx_t, U32)
        key_w = deal("key_w", key_w_picked, U32)
        gk_safe = sb("gk_safe", [P, PACK], F32, "key_w_picked")
        nc.vector.scalar_tensor_tensor(gk_safe[:], gk_t[:], 0.0, gk_t[:], ALU.is_equal, ALU.add)
        gk_inv = sb("gk_inv", [P, PACK], F32)
        nc.vector.reciprocal(gk_inv[:], gk_safe[:])
        gk_undo = sb("gk_undo", [P, PACK], F32)
        nc.gpsimd.tensor_scalar(gk_undo[:], gk_inv[:], 3.0e38, -3.0e38, ALU.min, ALU.max)

        s_ps = [psum.tile([P, S], F32, name="s_ps" + str(t), tag="high" + str(t)) for t in range(PACK)]
        for t in range(PACK):
            product(s_ps[t], (key_w, key_s), t, (xb_w, xb_s), whole, True, True)

        def part(offsets, u):
            return offsets[:, u * COLS : (u + 1) * COLS]

        y_plain = sb("y_plain", [P, PACK, S], F32)
        mix_win = four("mix_win", S)
        for t in range(PACK):
            nc.scalar.activation(y_win[t][:, :S], y_ps[t][:], ACT.Copy, scale=gn_t[:, t : t + 1])
            if t < 2:
                nc.sync.dma_start(y_plain[:, t, :], y_win[t][:, :S])
            else:
                nc.scalar.activation(y_plain[:, t, :], y_ps[t][:], ACT.Copy, scale=gn_t[:, t : t + 1])
        for t in (2, 3, 0, 1):
            for u in range(2):
                nc.vector.tensor_tensor(
                    mix_win[t][:, halves[u]], y_win[t][:].indirect(part(n1_t, u)), y_plain[:, t, halves[u]], ALU.subtract
                )

        s_plain = sb("s_plain", [P, PACK, S], F32)
        st2 = sb("st2", [P, PACK, S], F32)
        tanh_near = sb("tanh_near", [P, PACK, S], F32)
        for t in range(PACK):
            nc.scalar.activation(s_win[t][:, :S], s_ps[t][:], ACT.Copy, scale=gk_16th[:, t : t + 1])
            nc.sync.dma_start(s_plain[:, t, :], s_win[t][:, :S])
        mix_plain = sb("mix_plain", [P, PACK, S], F32, "gk_16th")
        for t in (2, 3, 0, 1):
            nc.sync.dma_start(mix_plain[:, t, :], mix_win[t][:])
        nc.scalar.copy(woven(w2_bf, halves[1]), planes(w2_raw[1][:]))
        for t in range(PACK):
            nc.vector.tensor_tensor(st2[:, t, :], s_win[t][:].indirect(n2_t[:]), s_plain[:, t, :], ALU.add)
        mix_near = sb("mix_near", [P, PACK, S], F32, "key_w")
        for t in (2, 3, 0, 1):
            for u in range(2):
                nc.scalar.activation(
                    mix_near[:, t, halves[u]], mix_win[t][:].indirect(part(n1_t, u)), ACT.Copy, scale=0.5
                )
        w3_raw = sb("w3_raw", [P, PACK, N], F32, "s_win0")
        nc.sync.dma_start(w3_raw[:], w3.rearrange("(p j) c -> p j c", j=PACK))
        w2_q = planes_for("w2")
        quantize(w2_q, w2_bf, whole)
        for t in range(PACK):
            nc.scalar.activation(tanh_win[t][:, :S], st2[:, t, :], ACT.Tanh, scale=gk_undo[:, t : t + 1])

        z_bf = [sb("z_bf" + str(u), [P, PACK * HALF], BF16, "s_win" + str(2 + u)) for u in range(2)]
        z_q = planes_for("z")
        for u in range(2):
            cols = halves[u]
            nc.vector.tensor_tensor(
                woven(z_bf[u], halves[0]), planes(mix_near[:, :, cols]), planes(mix_plain[:, :, cols]), ALU.subtract
            )
        for u in range(2):
            nc.vector.quantize_mx(out=z_q[0][:, halves[u]].bitcast(FP8X4), scales=z_q[1][:, halves[u]], in_=z_bf[u][:])
        w3_bf = sb("w3_bf", [P, PACK * N], BF16, "gk_16th")
        nc.vector.tensor_copy(woven(w3_bf, whole), planes(w3_raw[:]))
        w3_q = planes_for("w3")
        quantize(w3_q, w3_bf, whole)

        z2_q = planes_for("z2")
        h_ps = [
            [psum.tile([P, HALF], F32, name="h_ps" + tag + str(t), tag=tag + str(t)) for t in range(PACK)]
            for tag in ("low", "high")
        ]
        for u in range(2):
            for t in range(PACK):
                product(h_ps[u][t], w2_q, t, z_q, halves[u], True, False)
        for u in range(2):
            for t in range(PACK):
                nc.scalar.activation(tanh_near[:, t, halves[u]], tanh_win[t][:].indirect(part(n3_t, u)), ACT.Copy)
        for u in range(2):
            cols = halves[u]
            z2_bf = sb("z2_bf" + str(u), [P, PACK * HALF], BF16, "s_win" + str(2 + u))
            nc.vector.tensor_tensor(
                woven(z2_bf, halves[0]), planes(tanh_near[:, :, cols]), planes(st2[:, :, cols]), ALU.mult
            )
            nc.vector.quantize_mx(out=z2_q[0][:, cols].bitcast(FP8X4), scales=z2_q[1][:, cols], in_=z2_bf[:])
            for t in range(PACK):
                product(h_ps[u][t], w3_q, t, z2_q, cols, False, True)
            for t in range(PACK):
                if u == 1 and t == 1:
                    nc.vector.tensor_scalar(h_win[t][:, cols], h_ps[u][t][:], -0.5, None, ALU.mult)
                else:
                    nc.scalar.activation(h_win[t][:, cols], h_ps[u][t][:], ACT.Copy, scale=-0.5)

        h_near = sb("h_near", [P, PACK, S], F32)
        st3_near = sb("st3_near", [P, 2, S], F32)
        result = four("result", S)

        def store(t):
            nc.sync.dma_start(out[t * P : (t + 1) * P, :], result[t][:])

        def larger(t):
            nc.vector.scalar_tensor_tensor(st3_win[t][:, :S], h_win[t][:, :S], -2.0, h_near[:, t, :], ALU.mult, ALU.max)

        def fused_end(t):
            nc.vector.tensor_tensor(result[t][:], st3_win[t][:].indirect(n5_t[:]), h_win[t][:, :S], ALU.add)
            store(t)

        for t in range(PACK):
            if t == 1:
                nc.vector.tensor_copy(h_near[:, t, :], h_win[t][:].indirect(n4_t[:]))
            else:
                nc.scalar.activation(h_near[:, t, :], h_win[t][:].indirect(n4_t[:]), ACT.Copy, scale=-2.0)
        larger(0)
        for u in range(2):
            nc.vector.scalar_tensor_tensor(
                st3_win[1][:, halves[u]], h_near[:, 1, halves[u]], -2.0, h_ps[u][1][:], ALU.mult, ALU.max
            )
        fused_end(0)
        larger(2)
        larger(3)
        fused_end(2)
        for t in (1, 3):
            nc.scalar.activation(st3_near[:, t // 2, :], st3_win[t][:].indirect(n5_t[:]), ACT.Copy)
        nc.vector.tensor_tensor(result[1][:], st3_near[:, 0, :], h_win[1][:, :S], ALU.add)
        store(1)
        for cols in halves:
            nc.vector.tensor_tensor(result[3][:, cols], st3_near[:, 1, cols], h_win[3][:, cols], ALU.add)
            nc.sync.dma_start(out[3 * P :, cols], result[3][:, cols])
